import numpy as np, ml_dtypes
CORES = [10,34,74,98]
N = 4
BF = ml_dtypes.bfloat16
def gentries(a):
    return np.ascontiguousarray(a.reshape(8, 16, -1).transpose(0, 2, 1)).reshape(8, -1)
def gtable(e):
    e = np.asarray(e); return np.ascontiguousarray(e.reshape(8, -1, 16).transpose(0, 2, 1)).reshape(128, -1).astype(np.int32)
W, V, KC, R = 4096, 2048, 64, 3
LO, HI = 40, 250
def peps(rng):
    p = rng.integers(LO, HI + 1, (N, 8, V, 16)); i = np.arange(16); s = rng.integers(0, 15, (N, 8, V // 2, 1))
    p[:, :, 1::2] = np.take_along_axis(p[:, :, 0::2], np.where(i == s, s + 1, np.where(i == s + 1, s, i)), axis=-1); return p
def wants(rng):
    w = rng.integers(0, V, (N, 8, N, KC)); w[..., 1::2] = np.where(rng.random((N, 8, N, KC // 2)) < 0.25, w[..., 0::2] ^ 1, w[..., 1::2])
    w[..., KC - 1] = w[..., 2]; return w
def own(rng):
    e = np.argsort(rng.random((N, 8, V // 2)), axis=-1)[:, :, :N * KC // 2]; x = rng.integers(0, 2, e.shape)
    return np.stack([2 * e + x, 2 * e + 1 - x], axis=-1).reshape(N, 8, N, KC).transpose(2, 1, 0, 3).copy()
def bins(p, w):
    m = p[np.arange(N)[None, None, :, None], np.arange(8)[None, :, None, None], w].reshape(N, 8, N * KC, 16)
    b = np.add.accumulate(m, axis=-1); return b, b[..., -1:] + 64 - b
def noise(rng):
    return rng.integers(1, 4, (N, 8, 16, W)) * (rng.random((N, 8, 16, W)) < 0.3)
def some(rng):
    return np.argsort(rng.random((N, 8, N * KC)), axis=-1)[..., :R + 1]
def shine(rng, s, b, y, n, a, z):
    for r in range(N):
        for g in range(8):
            for t in n[r, g]:
                s[r, g][:, b[r, g, t]] = rng.integers(a, z + 1, (16, 16)); s[r, g][:, y[r, g, t]] = rng.integers(a, z + 1, (16, 16))
def pack(s, p, w):
    return {"spec": s.reshape(N, 128, W).astype(np.float32).astype(BF), "pep": p.transpose(0, 1, 3, 2).reshape(N, 128, V).astype(np.float32).astype(BF),
            "want": np.stack([gtable(w[r].reshape(8, N * KC)) for r in range(N)])}
def setup_inputs(rng):
    p, w, s, n = peps(rng), wants(rng), noise(rng), some(rng); b, y = bins(p, w)
    n[:, ::2, 0] = KC * rng.integers(0, N, (N, 4)) + 2; shine(rng, s, b, y, n, 4, 15)
    return pack(s, p, w)
def setup_inputs_kin(rng):
    p, w, s = peps(rng), own(rng), noise(rng); b, y = bins(p, w)
    n = 2 * np.argsort(rng.random((N, 8, N * KC // 2)), axis=-1)[..., :R + 1]
    shine(rng, s, b, y, n[..., 1:], 5, 9); shine(rng, s, b, y, n[..., :1], 12, 15)
    return pack(s, p, w)
def setup_inputs_twins(rng):
    p, w, s, n = peps(rng), own(rng), noise(rng), np.zeros((N, 8, 1), np.int64)
    for r in range(N):
        for g in range(8):
            q, k = [int(v) for v in rng.permutation(N)[:2]]; i, j = sorted([KC * q + int(rng.integers(KC)), KC * k + int(rng.integers(KC))])
            if g == 0: i, j = 0, N * KC - 1
            if g == 1: i = KC * q + int(rng.integers(KC - 1)); j = i + 1; w[r, g, q, j % KC] = w[r, g, q, i % KC]
            if g == 2: i, j = KC - 1, KC
            p[j // KC, g, w[r, g, j // KC, j % KC]] = p[i // KC, g, w[r, g, i // KC, i % KC]]; n[r, g, 0] = i
    b, y = bins(p, w); shine(rng, s, b, y, some(rng), 5, 9); shine(rng, s, b, y, n, 15, 15)
    s[:, 3] = rng.integers(1, 16, (N, 16, 1)); return pack(s, p, w)
def setup_inputs_ends(rng):
    p, w, s, n = peps(rng), wants(rng), noise(rng), np.zeros((N, 8, 1), np.int64)
    p[0, :, 0] = LO; p[N - 1, :, V - 1] = HI; p[:, :, 1] = 64; p[:, :, 2] = HI; p[:, :, 2, 0] = LO
    w[..., 0] = 0; w[..., 1] = 1; w[..., 2] = 2; w[..., KC - 1] = V - 1
    n[:, 0::4] = 1; n[:, 1::4] = 0; n[:, 2::4] = N * KC - 1; n[:, 3::4] = 2
    b, y = bins(p, w); shine(rng, s, b, y, some(rng), 5, 9); shine(rng, s, b, y, n, 15, 15)
    s[..., 0] = 15; s[..., W - 1] = 15; return pack(s, p, w)
def setup_inputs_dark(rng):
    p, w, s = peps(rng), own(rng), noise(rng)
    for r in range(N):
        for g in range(8): p[0, g, w[r, g, 0, 0], 0] = LO
    b, y = bins(p, w); shine(rng, s, b, y, some(rng), 4, 15)
    for r in range(N):
        d = rng.permutation(8)
        for g in d[:3]: s[r, g][:, y[r, g].reshape(-1)] = 0; s[r, g][:, LO] = rng.integers(1, 16, 16)
        s[r, d[3]] = 0
        g = d[4]; t = int(rng.integers(1, N * KC)); s[r, g][:, y[r, g].reshape(-1)] = 0
        s[r, g][:, b[r, g, t]] = rng.integers(8, 16, (16, 16)); s[r, g][:, y[r, g, t]] = rng.integers(8, 16, (16, 16))
    return pack(s, p, w)
def setup_inputs_spread(rng):
    p = np.minimum(HI, LO + ((HI - LO + 1) * rng.random((N, 8, V, 16)) ** 3).astype(np.int64)); k = (N, 8, 1, W)
    s = (rng.integers(0, 16, (N, 8, 16, W)) >> rng.integers(0, 3, k)) * (rng.random(k) > 0.0625)
    return pack(s, p, wants(rng))
def check_inputs(d):
    bad = []; s = d["spec"].astype(np.float32); p = d["pep"].astype(np.float32); w = d["want"]
    if not ((s >= 0) & (s <= 15) & (s == np.floor(s))).all(): bad.append("spec")
    if not ((p >= LO) & (p <= HI) & (p == np.floor(p))).all(): bad.append("pep")
    if not ((w >= 0) & (w < V)).all(): bad.append("want")
    return bad
def reference(spec, pep, want):
    left = spec.astype(np.float32).reshape(N, 8, 16, W); m_ = pep.astype(np.float32).astype(np.int64).reshape(N, 8, 16, V)
    win = np.zeros((N, 8, R), np.float32); score = np.zeros((N, 8, R), np.float32)
    for r in range(N):
        e = gentries(want[r]).reshape(8, N, KC)
        for g in range(8):
            m = np.concatenate([m_[q, g][:, e[g, q]] for q in range(N)], axis=1)
            b = np.add.accumulate(m, axis=0); y = b[15] + 64 - b
            s = left[r, g]
            for t in range(R):
                sc = np.sum(s[:, b] * s[:, y], axis=(0, 1))
                n = int(np.argmax(sc)); win[r, g, t] = n; score[r, g, t] = sc[n]
                s[:, b[:, n]] = 0; s[:, y[:, n]] = 0
    return {"win": win, "score": score, "left": left.reshape(N, 128, W).astype(BF)}

from concourse.bass import DstId, RemoteDMATransfer
from concourse.mybir import AluOpType, AxisListType, ActivationFunctionType

N, KC, W, V, R = 4, 64, 4096, 2048, 3
F = 288
YO = 64
FIRST = [(0, 16, True), (16, 32, False), (32, 64, False)]
LATER = [(0, 32, False), (32, 64, False)]

SCRATCH = {
    "wi": ("sbuf", [128, 16], "int32"),
    "wl": ("sbuf", [128, 16], "uint16"),
    "pepw": ("sbuf", [128, V], "bfloat16"),
    "sw": ("sbuf", [128, W], "bfloat16"),
    "ones": ("sbuf", [128, 128], "bfloat16"),
    "blk": ("sbuf", [128, 128], "bfloat16"),
    "lb": ("sbuf", [128, 128], "bfloat16"),
    "ly": ("sbuf", [128, 128], "bfloat16"),
    "wf": ("sbuf", [128, 128], "bfloat16"),
    "idx": ("sbuf", [128, 256], "bfloat16"),
    "zer": ("sbuf", [128, 16], "bfloat16"),
    "pg": ("sbuf", [128, 256], "bfloat16"),
    "yg": ("sbuf", [128, W], "bfloat16"),
    "pr": ("sbuf", [128, W], "bfloat16"),
    "tab": ("sbuf", [128, 512], "float32"),
    "nk": ("sbuf", [128, 4], "float32"),
    "hi": ("sbuf", [128, 4], "int32"),
    "co": ("sbuf", [128, 8], "uint16"),
    "wb": ("sbuf", [128, 16], "uint16"),
    "wy": ("sbuf", [128, 16], "uint16"),
    "winf": ("sbuf", [128, 4], "float32"),
    "scf": ("sbuf", [128, 4], "float32"),
    "key": ("psum", [128, 512], "float32"),
}
for _q in range(N):
    SCRATCH["lst%d" % _q] = ("sbuf", [128, 16], "uint16")
    SCRATCH["off%d" % _q] = ("sbuf", [128, 128], "uint16")
    SCRATCH["rep%d" % _q] = ("sbuf", [128, 128], "uint16")
    SCRATCH["ps%d" % _q] = ("psum", [128, 512], "float32")

SEMAPHORES = (["ldw", "ldp", "lds", "conv", "vone", "vzer", "gb1", "gb2", "glb", "gix", "vly", "swf", "go", "lsent",
               "rsent", "offr", "tabs", "yd", "pk", "red", "hs", "cs", "ws", "k1", "k2", "fin", "stl", "sts"]
              + ["lst%d" % q for q in range(N)] + ["rp%d" % q for q in range(N)]
              + ["pg%d" % q for q in range(N)] + ["po%d" % q for q in range(N)]
              + ["rc%d" % q for q in range(N)] + ["pb%d" % q for q in range(N)]
              + ["y%d" % k for k in range(10)])


def rank_program(g, core, T, topo):
    rank = T.rank_of(core)
    if rank is None:
        return
    S = T.sem
    v, act, pe, sp = g.vector, g.scalar, g.tensor, g.sync
    op = AluOpType
    copy = ActivationFunctionType.Copy
    cores = T.cores

    def far(q):
        return 0 if topo.same_plane(topo.chip(cores[q]), topo.chip(core)) else 1

    others = [q for q in range(N) if q != rank]
    sends = sorted(others, key=lambda q: (far(q), (q - rank) % N))
    order = [rank] + sorted(others, key=lambda q: (far(q), (rank - q) % N))
    nin = {q: len(topo.engines(cores[q], core)) for q in others}
    mask = topo.mask(core, cores[others[0]])
    for q in others:
        mask &= topo.mask(core, cores[q])
    nall = len([e for e in topo.engines(core, cores[others[0]]) if mask >> e & 1])

    off = [T["off%d" % q] for q in range(N)]
    ps = [T["ps%d" % q] for q in range(N)]

    pieces = []
    for b, q in enumerate(order):
        for (a, z, mine) in (FIRST if b == 0 else LATER):
            pieces.append((b, q, a, z, mine, len(pieces)))
    count = [len([p for p in pieces if p[0] == b]) for b in range(N)]

    sp.dma_start(T.wi[:], T.want[:]).then_inc(S.ldw, 16)
    sp.dma_start(T.pepw[:], T.pep[:]).then_inc(S.ldp, 16)
    sp.wait_ge(S.go, 1)
    sp.dma_start(T.sw[:], T.spec[:]).then_inc(S.lds, 16)

    g.wait_ge(S.vone, 1)
    g.affine_select(T.blk[:], T.ones[:], [[-16, 8], [0, 16]], op.is_ge, 0.0, 0, 1).then_inc(S.gb1, 1)
    g.wait_ge(S.gb1, 1)
    g.affine_select(T.blk[:], T.blk[:], [[16, 8], [0, 16]], op.is_ge, 0.0, 15, -1).then_inc(S.gb2, 1)
    g.wait_ge(S.gb2, 1)
    g.affine_select(T.lb[:], T.blk[:], [[1, 128]], op.is_ge, 0.0, 0, -1).then_inc(S.glb, 1)
    g.wait_ge(S.conv, 1)
    ids = []
    for q in sends:
        rid, pid, _ = topo.addr(cores[q])
        ids.append(DstId(rid=rid, pnc=pid))
    land = T["lst%d" % rank]
    g.remote_dma_fused([RemoteDMATransfer(dst_ids=ids, dma_engine_mask=mask, remote_sem=S["lst%d" % rank],
                                          srcs=[T.wl[:]], dsts=[land[:] for q in sends])], local_sem=S.lsent)
    g.sem_inc(S.go, 1)
    g.iota(T.idx[0:1, 0:256], [[-1, 256]], 0, 0, allow_small_or_imprecise_dtypes=True).then_inc(S.gix, 1)
    total = 0
    for q in sends:
        g.wait_ge(S["rc%d" % q], 1)
        rid, pid, _ = topo.addr(cores[q])
        g.remote_dma(off[rank][:], T["rep%d" % q][:], S["rp%d" % rank], S.rsent, pid, rid, topo.mask(core, cores[q]))
        total += len(topo.engines(core, cores[q]))

    def bins_mm(q, slot):
        pe.wait_ge(S["pg%d" % q], 1)
        G = T.pg[:, KC * slot:KC * slot + KC]
        pe.matmul(ps[q][:, 0:KC], T.lb[:], G, True, True)
        pe.matmul(ps[q][:, KC:2 * KC], T.ly[:], G, True, True).then_inc(S["po%d" % q], 1)

    pe.wait_ge(S.glb, 1)
    pe.wait_ge(S.vly, 1)
    bins_mm(rank, 0)
    for s, q in enumerate(sends):
        bins_mm(q, s + 1)
    pe.wait_ge(S.swf, 1)
    pe.wait_ge(S.gix, 1)
    for t in range(R):
        if t:
            pe.wait_ge(S.red, t)
        for b, q in enumerate(order):
            dst = T.key[:, KC * q:KC * q + KC]
            pe.matmul(dst, T.ones[0:1, 0:128], T.idx[0:1, KC * q:KC * q + KC], True, False)
            pe.wait_ge(S["pb%d" % b], count[b] * (t + 1))
            for i in range(16):
                mm = pe.matmul(dst, T.wf[:], T.pr[:, 1024 * b + i:1024 * (b + 1):16], False, i == 15)
            mm.then_inc(S.pk, 1)

    act.wait_ge(S.gb2, 1)
    act.activation(T.wf[:], T.blk[:], copy, scale=float(F)).then_inc(S.swf, 1)
    for t in range(R):
        seen = []
        if t == 0:
            act.wait_ge(S.lds, 16)
        else:
            act.wait_ge(S.k2, t)
        for (b, q, a, z, mine, k) in pieces:
            if mine:
                continue
            if t == 0 and q not in seen:
                seen.append(q)
                if q == rank:
                    act.wait_ge(S.offr, 1)
                else:
                    act.wait_ge(S["rp%d" % q], nin[q])
            act.activation(T.yg[:, 1024 * b + 16 * a:1024 * b + 16 * z],
                           T.sw[:, YO:W].indirect(off[q][:, KC + a:KC + z]), copy).then_inc(S["y%d" % k], 1)

    v.memset(T.ones[:], 1.0).then_inc(S.vone, 1)
    v.memset(T.zer[:], 0.0).then_inc(S.vzer, 1)
    v.wait_ge(S.ldw, 16)
    v.tensor_copy(T.wl[:], T.wi[:]).then_inc(S.conv, 1)
    v.wait_ge(S.conv, 1)
    v.wait_ge(S.ldp, 16)
    v.tensor_copy(T.pg[:, 0:KC], T.pepw[:].indirect(T.wl[:, 4 * rank:4 * rank + 4])).then_inc(S["pg%d" % rank], 1)
    v.wait_ge(S.glb, 1)
    v.tensor_tensor(T.ly[:], T.blk[:], T.lb[:], op.subtract).then_inc(S.vly, 1)
    v.wait_ge(S["po%d" % rank], 1)
    v.tensor_copy(off[rank][:], ps[rank][:, 0:2 * KC]).then_inc(S.offr, 1)

    def pick(q, slot):
        v.wait_ge(S["lst%d" % q], nin[q])
        v.tensor_copy(T.pg[:, KC * slot:KC * slot + KC],
                      T.pepw[:].indirect(T["lst%d" % q][:, 4 * rank:4 * rank + 4])).then_inc(S["pg%d" % q], 1)

    def pack(q):
        v.wait_ge(S["po%d" % q], 1)
        v.tensor_copy(T["rep%d" % q][:], ps[q][:, 0:2 * KC]).then_inc(S["rc%d" % q], 1)

    pick(sends[0], 1)
    pack(sends[0])
    pick(sends[1], 2)
    pick(sends[2], 3)
    pack(sends[1])
    pack(sends[2])
    v.wait_ge(S.offr, 1)
    v.wait_ge(S.lds, 16)
    v.wait_ge(S.vzer, 1)
    for t in range(R):
        for (b, q, a, z, mine, k) in pieces:
            y = T.yg[:, 1024 * b + 16 * a:1024 * b + 16 * z]
            if mine:
                v.tensor_copy(y, T.sw[:, YO:W].indirect(off[q][:, KC + a:KC + z])).then_inc(S.yd, 1)
                v.wait_ge(S.yd, t + 1)
            else:
                v.wait_ge(S["y%d" % k], t + 1)
            v.tensor_tensor(T.pr[:, 1024 * b + 16 * a:1024 * b + 16 * z], T.sw[:].indirect(off[q][:, a:z]), y,
                            op.mult).then_inc(S["pb%d" % b], 1)
        if t == 0:
            for q in range(N):
                v.tensor_copy(T.tab[:, KC * q:KC * q + KC], off[q][:, 0:KC]).then_inc(S.tabs, 1)
                v.tensor_copy(T.tab[:, 256 + KC * q:256 + KC * q + KC], off[q][:, KC:2 * KC]).then_inc(S.tabs, 1)
            v.wait_ge(S.tabs, 2 * N)
        v.wait_ge(S.pk, N * (t + 1))
        v.tensor_reduce(T.nk[:, t:t + 1], T.key[:, 0:256], AxisListType.X, op.max, negate=True).then_inc(S.red, 1)
        v.wait_ge(S.red, t + 1)
        v.tensor_scalar(T.hi[:, t:t + 1], T.nk[:, t:t + 1], -128.0, 1.0 / F, op.add, op.mult).then_inc(S.hs, 1)
        v.wait_ge(S.hs, t + 1)
        v.tensor_scalar(T.co[:, 2 * t:2 * t + 1], T.hi[:, t:t + 1], -float(F), T.nk[:, t:t + 1],
                        op.mult, op.add).then_inc(S.cs, 1)
        v.wait_ge(S.cs, t + 1)
        pos = T.co[:, 2 * t:2 * t + 1]
        v.tensor_copy(T.wb[:], T.tab[:, 0:256].indirect(pos)).then_inc(S.ws, 1)
        v.tensor_copy(T.wy[:], T.tab[:, 256:512].indirect(pos)).then_inc(S.ws, 1)
        v.wait_ge(S.ws, 2 * (t + 1))
        v.tensor_copy(T.sw[:].indirect(T.wb[:, 0:1]), T.zer[:]).then_inc(S.k1, 1)
        v.wait_ge(S.k1, t + 1)
        v.tensor_copy(T.sw[:, YO:W].indirect(T.wy[:, 0:1]), T.zer[:]).then_inc(S.k2, 1)
        if t < R - 1:
            v.wait_ge(S.k2, t + 1)
    v.tensor_copy(T.winf[:, 0:R], T.co[:, 0:2 * R:2]).then_inc(S.fin, 1)
    v.tensor_scalar(T.scf[:, 0:R], T.hi[:, 0:R], -1.0, None, op.mult).then_inc(S.fin, 1)

    sp.wait_ge(S.k2, R)
    sp.dma_start(T.left[:], T.sw[:]).then_inc(S.stl, 16)
    act.wait_ge(S.fin, 2)
    act.dma_start(T.win[:], T.winf[0:128:16, 0:R]).then_inc(S.sts, 16)
    act.dma_start(T.score[:], T.scf[0:128:16, 0:R]).then_inc(S.sts, 16)
    sp.wait_ge(S.stl, 16)
    act.wait_ge(S.sts, 32)
    g.wait_ge(S.lsent, nall)
    g.wait_ge(S.rsent, total)
